import numpy as np
import ml_dtypes


def mxq(x, axis, fmt="e4m3"):
    dtype, down = {"e4m3": (ml_dtypes.float8_e4m3fn, 7), "e5m2": (ml_dtypes.float8_e5m2, 14)}[fmt]
    v = np.moveaxis(np.asarray(x, np.float32).astype(ml_dtypes.bfloat16).astype(np.float64), axis, -1)
    blocks = v.reshape(v.shape[:-1] + (-1, 32))
    amax = np.abs(blocks).max(-1, keepdims=True)
    byte = np.maximum(np.where(amax > 0, np.frexp(amax)[1] - 1 + 127, 0) - down, 1)
    scale = np.exp2(byte - 127.0)
    codes = (blocks / scale).astype(np.float32).astype(dtype).astype(np.float64)
    return np.moveaxis((codes * scale).reshape(v.shape), -1, axis)


WIDE = False


def mx_kscale(k):
    if not WIDE:
        return np.ones(k)
    levels = np.array([10, -10, 5, -5, 0])
    if k % 512:
        return np.exp2(np.random.permutation(np.resize(levels, k // 32))).repeat(32)
    a = np.empty((k // 512, 16))
    for p in range(k // 512):
        a[p, :8] = np.random.permutation(np.resize(levels, 8))
        for g in range(8):
            far = levels[np.abs(levels - a[p, g]) >= 10]
            a[p, g + 8] = far[np.random.randint(len(far))]
    return np.exp2(a.ravel()).repeat(32)


def f64(x):
    return np.asarray(x).astype(np.float64)


def striped(idx):
    return np.tile(idx.reshape(-1, 16).T, (8, 1)).astype(np.uint16)


def unstriped(offs):
    return offs[:16].T.reshape(-1).astype(np.int64)


K, T, S, H, N, U = 512, 2048, 512, 512, 256, 1024


def setup_inputs():
    n = np.random.standard_normal
    s = mx_kscale(K)[:, None]
    u = mx_kscale(H)
    return {
        "xT": (n((K, T)) * s).astype(np.float32),
        "w1": (n((K, H)) / np.sqrt(K) / s * u).astype(np.float32),
        "w2": (n((H, N)) / np.sqrt(H) / u[:, None]).astype(np.float32),
        "skip": (n((H, U)) * u[:, None]).astype(np.float32),
        "offs": striped(np.random.permutation(T)[:S]),
        "cell": striped(np.random.permutation(U)[:S]),
    }


def reference(xT, w1, w2, skip, offs, cell):
    xq = mxq(f64(xT)[:, unstriped(offs)], 0, "e4m3")
    up = np.zeros((H, U))
    up[:, unstriped(cell)] = mxq(f64(w1), 0, "e4m3").T @ xq
    z = up + f64(skip)
    return mxq(f64(w2), 0, "e4m3").T @ mxq(z, 0, "e4m3")

@@ -1,0 +1,157 @@
+from contextlib import ExitStack
+
+import concourse.mybir as mybir
+
+K, T, S, H, N, U = 512, 2048, 512, 512, 256, 1024
+FLOPS = 2 * K * H * S + 2 * H * N * U
+
+F32 = mybir.dt.float32
+BF16 = mybir.dt.bfloat16
+U32 = mybir.dt.uint32
+U16 = mybir.dt.uint16
+U8 = mybir.dt.uint8
+FP8X4 = mybir.dt.float8_e4m3fn_x4
+ADD = mybir.AluOpType.add
+
+P = 128
+PACK = 4
+STRIPE = 16
+HALF = S // 2
+CHUNK = 256
+CHUNKS = U // CHUNK
+
+
+def tile_picked_unet_none_e_kernel(tc, xT, w1, w2, skip, offs, cell, out):
+    nc = tc.nc
+    with ExitStack() as ctx:
+        keep = ctx.enter_context(tc.tile_pool(name="keep", bufs=1))
+        hpsum = ctx.enter_context(tc.psum_pool(name="hpsum", bufs=1))
+        opsum = ctx.enter_context(tc.psum_pool(name="opsum", bufs=3))
+
+        def quantise(codes, scales, grouped):
+            nc.vector.quantize_mx(out=codes.bitcast(FP8X4), scales=scales, in_=grouped)
+
+        offs_sb = keep.tile([P, S // STRIPE], U16, name="offs_sb")
+        cell_sb = keep.tile([P, S // STRIPE], U16, name="cell_sb")
+        x_rows = xT.rearrange("(p j) t -> j p t", j=PACK)
+        skip_rows = skip.rearrange("(p j) v -> j p v", j=PACK)
+        x_plane = [keep.tile([P, T], F32, name=f"x_plane{j}") for j in range(PACK)]
+        skip_plane = [keep.tile([P, U], F32, name=f"skip_plane{j}") for j in range(PACK)]
+        w1_raw = keep.tile([P, PACK, H], F32, name="w1_raw")
+        w2_raw = keep.tile([P, PACK, N], F32, name="w2_raw")
+
+        nc.sync.dma_start(x_plane[0][:], x_rows[0])
+        nc.sync.dma_start(offs_sb[:], offs)
+        nc.sync.dma_start(w1_raw[:], w1.rearrange("(p j) c -> p j c", j=PACK))
+        for j in range(1, PACK):
+            nc.sync.dma_start(x_plane[j][:], x_rows[j])
+        nc.sync.dma_start(cell_sb[:], cell)
+        nc.sync.dma_start(skip_plane[0][:], skip_rows[0])
+        nc.sync.dma_start(skip_plane[1][:], skip_rows[1])
+        nc.sync.dma_start(w2_raw[:], w2.rearrange("(p j) m -> p j m", j=PACK))
+        nc.sync.dma_start(skip_plane[2][:], skip_rows[2])
+        nc.sync.dma_start(skip_plane[3][:], skip_rows[3])
+
+        up = [keep.tile([P, U], F32, name=f"up{t}") for t in range(PACK)]
+        for t in range(PACK):
+            nc.vector.memset(up[t][:], 0.0)
+
+        w1_grouped = keep.tile([P, PACK, P, PACK], BF16, name="w1_grouped", align_bytes=64)
+        nc.scalar.copy(
+            out=w1_grouped[:].rearrange("p t m j -> p m j t"),
+            in_=w1_raw[:].rearrange("p j (m t) -> p m j t", t=PACK),
+        )
+        w1_codes = keep.tile([P, H], U32, name="w1_codes", align_bytes=64)
+        w1_scales = keep.tile([P, H], U8, name="w1_scales", align_bytes=64)
+
+        x_grouped = [keep.tile([P, HALF, PACK], BF16, name=f"x_grouped{a}", align_bytes=64) for a in range(2)]
+        x_codes = keep.tile([P, S], U32, name="x_codes", align_bytes=64)
+        x_scales = keep.tile([P, S], U8, name="x_scales", align_bytes=64)
+        list_cols = [slice(a * HALF // STRIPE, (a + 1) * HALF // STRIPE) for a in range(2)]
+        entries = [slice(a * HALF, (a + 1) * HALF) for a in range(2)]
+        for j in range(PACK):
+            for a in range(2):
+                nc.vector.tensor_copy(x_grouped[a][:, :, j], x_plane[j][:].indirect(offs_sb[:, list_cols[a]]))
+            if j == 0:
+                quantise(w1_codes[:], w1_scales[:], w1_grouped[:].rearrange("p t m j -> p (t m j)"))
+        for a in range(2):
+            quantise(x_codes[:, entries[a]], x_scales[:, entries[a]], x_grouped[a][:].rearrange("p s j -> p (s j)"))
+
+        def product(acc, w_codes, w_scales, w_cols, codes, scales, cols):
+            nc.tensor.matmul_mx(
+                out=acc,
+                lhsT=w_codes[:, w_cols].bitcast(FP8X4),
+                lhsT_scale=w_scales[:, w_cols],
+                rhs=codes[:, cols].bitcast(FP8X4),
+                rhs_scale=scales[:, cols],
+                start=True,
+                stop=True,
+            )
+
+        h_sb = [keep.tile([P, S], F32, name=f"h_sb{t}") for t in range(PACK)]
+        pieces = [(0, slice(0, HALF)), (0, slice(HALF, S))] + [(t, slice(0, S)) for t in range(1, PACK)]
+        for n, (t, cols) in enumerate(pieces):
+            acc = hpsum.tile([P, cols.stop - cols.start], F32, name=f"h_acc{n}")
+            product(acc[:], w1_codes, w1_scales, slice(t * P, (t + 1) * P), x_codes, x_scales, cols)
+            nc.scalar.copy(out=h_sb[t][:, cols], in_=acc[:])
+
+        w2_grouped = keep.tile([P, N, PACK], BF16, name="w2_grouped", align_bytes=64)
+        nc.scalar.copy(
+            out=w2_grouped[:].rearrange("p (c i) j -> p c j i", i=4),
+            in_=w2_raw[:].rearrange("p j (c i) -> p c j i", i=4),
+        )
+        w2_codes = keep.tile([P, N], U32, name="w2_codes", align_bytes=64)
+        w2_scales = keep.tile([P, N], U8, name="w2_scales", align_bytes=64)
+
+        z_low = keep.tile([P, 2, U], BF16, name="z_low")
+        z_high = [keep.tile([P, 2, CHUNK], BF16, name=f"z_high{c}") for c in range(CHUNKS)]
+        z_grouped = [keep.tile([P, CHUNK, PACK], BF16, name=f"z_grouped{c}", align_bytes=64) for c in range(CHUNKS)]
+        cells = [slice(c * CHUNK, (c + 1) * CHUNK) for c in range(CHUNKS)]
+
+        def scatter(t, cols):
+            lst = cell_sb[:, cols.start // STRIPE : cols.stop // STRIPE]
+            nc.vector.tensor_copy(up[t][:].indirect(lst), h_sb[t][:, cols])
+
+        for t, cols in pieces:
+            scatter(t, cols)
+            if cols.stop < S:
+                continue
+            if t < 2:
+                nc.vector.tensor_tensor(z_low[:, t, :], up[t][:], skip_plane[t][:], ADD)
+            if t == 1:
+                quantise(w2_codes[:], w2_scales[:], w2_grouped[:].rearrange("p m j -> p (m j)"))
+                for c in range(CHUNKS):
+                    nc.scalar.copy(
+                        out=z_grouped[c][:, :, 0:2],
+                        in_=z_low[:, :, cells[c]].rearrange("p e v -> p v e"),
+                    )
+            if t == 2:
+                for c in range(CHUNKS):
+                    nc.vector.tensor_tensor(z_high[c][:, 0, :], up[t][:, cells[c]], skip_plane[t][:, cells[c]], ADD)
+
+        z_codes = [keep.tile([P, CHUNK], U32, name=f"z_codes{c}", align_bytes=64) for c in range(CHUNKS)]
+        z_scales = [keep.tile([P, CHUNK], U8, name=f"z_scales{c}", align_bytes=64) for c in range(CHUNKS)]
+        out_rows = out.rearrange("(m p) v -> p m v", p=P)
+
+        def add_last(c):
+            nc.vector.tensor_tensor(z_high[c][:, 1, :], up[3][:, cells[c]], skip_plane[3][:, cells[c]], ADD)
+
+        def weave(c):
+            nc.vector.tensor_copy(z_grouped[c][:, :, 2:4], z_high[c][:].rearrange("p e v -> p v e"))
+
+        def finish(c):
+            quantise(z_codes[c][:], z_scales[c][:], z_grouped[c][:].rearrange("p v j -> p (v j)"))
+            acc = opsum.tile([P, 2, CHUNK], F32, name="o_acc")
+            for m in range(2):
+                product(acc[:, m, :], w2_codes, w2_scales, slice(m * P, (m + 1) * P), z_codes[c], z_scales[c], slice(0, CHUNK))
+            result = keep.tile([P, 2, CHUNK], F32, name=f"result{c}")
+            nc.scalar.copy(out=result[:], in_=acc[:])
+            nc.sync.dma_start(out_rows[:, :, cells[c]], result[:])
+
+        for step in range(CHUNKS + 2):
+            if step < CHUNKS:
+                add_last(step)
+            if 1 <= step <= CHUNKS:
+                weave(step - 1)
+            if step >= 2:
+                finish(step - 2)

@@ -17,16 +17,16 @@ P = 128
 PACK = 4
 STRIPE = 16
 HALF = S // 2
-CHUNK = 256
-CHUNKS = U // CHUNK
+GRAIN = 128
+WIDTHS = (2, 2, 2, 1, 1)
+CHUNKS = len(WIDTHS)
 
 
 def tile_picked_unet_none_e_kernel(tc, xT, w1, w2, skip, offs, cell, out):
     nc = tc.nc
     with ExitStack() as ctx:
         keep = ctx.enter_context(tc.tile_pool(name="keep", bufs=1))
-        hpsum = ctx.enter_context(tc.psum_pool(name="hpsum", bufs=1))
-        opsum = ctx.enter_context(tc.psum_pool(name="opsum", bufs=3))
+        psum = ctx.enter_context(tc.psum_pool(name="psum", bufs=8))
 
         def quantise(codes, scales, grouped):
             nc.vector.quantize_mx(out=codes.bitcast(FP8X4), scales=scales, in_=grouped)
@@ -37,14 +37,16 @@ def tile_picked_unet_none_e_kernel(tc, xT, w1, w2, skip, offs, cell, out):
         skip_rows = skip.rearrange("(p j) v -> j p v", j=PACK)
         x_plane = [keep.tile([P, T], F32, name=f"x_plane{j}") for j in range(PACK)]
         skip_plane = [keep.tile([P, U], F32, name=f"skip_plane{j}") for j in range(PACK)]
-        w1_raw = keep.tile([P, PACK, H], F32, name="w1_raw")
+        w1_raw = [keep.tile([P, 2, H], F32, name=f"w1_raw{u}") for u in range(2)]
         w2_raw = keep.tile([P, PACK, N], F32, name="w2_raw")
 
         nc.sync.dma_start(x_plane[0][:], x_rows[0])
         nc.sync.dma_start(offs_sb[:], offs)
-        nc.sync.dma_start(w1_raw[:], w1.rearrange("(p j) c -> p j c", j=PACK))
+        w1_rows = w1.rearrange("(p j) c -> p j c", j=PACK)
+        nc.sync.dma_start(w1_raw[0][:], w1_rows[:, 0:2, :])
         for j in range(1, PACK):
             nc.sync.dma_start(x_plane[j][:], x_rows[j])
+        nc.sync.dma_start(w1_raw[1][:], w1_rows[:, 2:4, :])
         nc.sync.dma_start(cell_sb[:], cell)
         nc.sync.dma_start(skip_plane[0][:], skip_rows[0])
         nc.sync.dma_start(skip_plane[1][:], skip_rows[1])
@@ -56,13 +58,12 @@ def tile_picked_unet_none_e_kernel(tc, xT, w1, w2, skip, offs, cell, out):
         for t in range(PACK):
             nc.vector.memset(up[t][:], 0.0)
 
-        w1_grouped = keep.tile([P, PACK, P, PACK], BF16, name="w1_grouped", align_bytes=64)
-        nc.scalar.copy(
-            out=w1_grouped[:].rearrange("p t m j -> p m j t"),
-            in_=w1_raw[:].rearrange("p j (m t) -> p m j t", t=PACK),
-        )
-        w1_codes = keep.tile([P, H], U32, name="w1_codes", align_bytes=64)
-        w1_scales = keep.tile([P, H], U8, name="w1_scales", align_bytes=64)
+        w1_grouped = [keep.tile([P, P, PACK], BF16, name=f"w1_grouped{t}", align_bytes=64) for t in range(PACK)]
+        w1_codes = [keep.tile([P, P], U32, name=f"w1_codes{t}", align_bytes=64) for t in range(PACK)]
+        w1_scales = [keep.tile([P, P], U8, name=f"w1_scales{t}", align_bytes=64) for t in range(PACK)]
+        w1_dealt = [raw[:].rearrange("p e (m t) -> p t m e", t=PACK) for raw in w1_raw]
+        for t in range(PACK):
+            nc.scalar.copy(out=w1_grouped[t][:, :, 0:2], in_=w1_dealt[0][:, t])
 
         x_grouped = [keep.tile([P, HALF, PACK], BF16, name=f"x_grouped{a}", align_bytes=64) for a in range(2)]
         x_codes = keep.tile([P, S], U32, name="x_codes", align_bytes=64)
@@ -72,10 +73,18 @@ def tile_picked_unet_none_e_kernel(tc, xT, w1, w2, skip, offs, cell, out):
         for j in range(PACK):
             for a in range(2):
                 nc.vector.tensor_copy(x_grouped[a][:, :, j], x_plane[j][:].indirect(offs_sb[:, list_cols[a]]))
-            if j == 0:
-                quantise(w1_codes[:], w1_scales[:], w1_grouped[:].rearrange("p t m j -> p (t m j)"))
-        for a in range(2):
+
+        def quantise_x(a):
             quantise(x_codes[:, entries[a]], x_scales[:, entries[a]], x_grouped[a][:].rearrange("p s j -> p (s j)"))
+
+        def quantise_w1(t):
+            nc.scalar.copy(out=w1_grouped[t][:, :, 2:4], in_=w1_dealt[1][:, t])
+            quantise(w1_codes[t][:], w1_scales[t][:], w1_grouped[t][:].rearrange("p m j -> p (m j)"))
+
+        quantise_x(0)
+        quantise_w1(0)
+        quantise_x(1)
+        quantise_w1(1)
 
         def product(acc, w_codes, w_scales, w_cols, codes, scales, cols):
             nc.tensor.matmul_mx(
@@ -91,9 +100,11 @@ def tile_picked_unet_none_e_kernel(tc, xT, w1, w2, skip, offs, cell, out):
         h_sb = [keep.tile([P, S], F32, name=f"h_sb{t}") for t in range(PACK)]
         pieces = [(0, slice(0, HALF)), (0, slice(HALF, S))] + [(t, slice(0, S)) for t in range(1, PACK)]
         for n, (t, cols) in enumerate(pieces):
-            acc = hpsum.tile([P, cols.stop - cols.start], F32, name=f"h_acc{n}")
-            product(acc[:], w1_codes, w1_scales, slice(t * P, (t + 1) * P), x_codes, x_scales, cols)
-            nc.scalar.copy(out=h_sb[t][:, cols], in_=acc[:])
+            if t >= 2:
+                quantise_w1(t)
+            acc = psum.tile([P, S], F32, name="acc")
+            product(acc[:, cols], w1_codes[t], w1_scales[t], slice(0, P), x_codes, x_scales, cols)
+            nc.scalar.copy(out=h_sb[t][:, cols], in_=acc[:, cols])
 
         w2_grouped = keep.tile([P, N, PACK], BF16, name="w2_grouped", align_bytes=64)
         nc.scalar.copy(
@@ -103,10 +114,16 @@ def tile_picked_unet_none_e_kernel(tc, xT, w1, w2, skip, offs, cell, out):
         w2_codes = keep.tile([P, N], U32, name="w2_codes", align_bytes=64)
         w2_scales = keep.tile([P, N], U8, name="w2_scales", align_bytes=64)
 
+        grains = U // GRAIN
+        firsts = [sum(WIDTHS[:c]) for c in range(CHUNKS)]
+        spans = [slice(firsts[c], firsts[c] + WIDTHS[c]) for c in range(CHUNKS)]
+        cells = [slice(s.start * GRAIN, s.stop * GRAIN) for s in spans]
         z_low = keep.tile([P, 2, U], BF16, name="z_low")
-        z_high = [keep.tile([P, 2, CHUNK], BF16, name=f"z_high{c}") for c in range(CHUNKS)]
-        z_grouped = [keep.tile([P, CHUNK, PACK], BF16, name=f"z_grouped{c}", align_bytes=64) for c in range(CHUNKS)]
-        cells = [slice(c * CHUNK, (c + 1) * CHUNK) for c in range(CHUNKS)]
+        z_high = keep.tile([P, grains, 2, GRAIN], BF16, name="z_high")
+        z_grouped = [keep.tile([P, WIDTHS[c] * GRAIN, PACK], BF16, name=f"z_grouped{c}", align_bytes=64) for c in range(CHUNKS)]
+
+        def by_grain(ap):
+            return ap.rearrange("p (g v) -> p g v", v=GRAIN)
 
         def scatter(t, cols):
             lst = cell_sb[:, cols.start // STRIPE : cols.stop // STRIPE]
@@ -117,7 +134,7 @@ def tile_picked_unet_none_e_kernel(tc, xT, w1, w2, skip, offs, cell, out):
             if cols.stop < S:
                 continue
             if t < 2:
-                nc.vector.tensor_tensor(z_low[:, t, :], up[t][:], skip_plane[t][:], ADD)
+                nc.gpsimd.tensor_tensor(z_low[:, t, :], up[t][:], skip_plane[t][:], ADD)
             if t == 1:
                 quantise(w2_codes[:], w2_scales[:], w2_grouped[:].rearrange("p m j -> p (m j)"))
                 for c in range(CHUNKS):
@@ -126,26 +143,40 @@ def tile_picked_unet_none_e_kernel(tc, xT, w1, w2, skip, offs, cell, out):
                         in_=z_low[:, :, cells[c]].rearrange("p e v -> p v e"),
                     )
             if t == 2:
-                for c in range(CHUNKS):
-                    nc.vector.tensor_tensor(z_high[c][:, 0, :], up[t][:, cells[c]], skip_plane[t][:, cells[c]], ADD)
+                nc.gpsimd.tensor_tensor(z_high[:, :, 0, :], by_grain(up[t][:]), by_grain(skip_plane[t][:]), ADD)
 
-        z_codes = [keep.tile([P, CHUNK], U32, name=f"z_codes{c}", align_bytes=64) for c in range(CHUNKS)]
-        z_scales = [keep.tile([P, CHUNK], U8, name=f"z_scales{c}", align_bytes=64) for c in range(CHUNKS)]
+        z_codes = [keep.tile([P, WIDTHS[c] * GRAIN], U32, name=f"z_codes{c}", align_bytes=64) for c in range(CHUNKS)]
+        z_scales = [keep.tile([P, WIDTHS[c] * GRAIN], U8, name=f"z_scales{c}", align_bytes=64) for c in range(CHUNKS)]
         out_rows = out.rearrange("(m p) v -> p m v", p=P)
 
         def add_last(c):
-            nc.vector.tensor_tensor(z_high[c][:, 1, :], up[3][:, cells[c]], skip_plane[3][:, cells[c]], ADD)
+            nc.vector.tensor_tensor(z_high[:, spans[c], 1, :], by_grain(up[3][:, cells[c]]), by_grain(skip_plane[3][:, cells[c]]), ADD)
 
         def weave(c):
-            nc.vector.tensor_copy(z_grouped[c][:, :, 2:4], z_high[c][:].rearrange("p e v -> p v e"))
+            dst = z_grouped[c][:, :, 2:4].rearrange("p (g v) e -> p g v e", v=GRAIN)
+            src = z_high[:, spans[c], :, :].rearrange("p g e v -> p g v e")
+            if c == 1:
+                nc.scalar.copy(out=dst, in_=src)
+            else:
+                nc.vector.tensor_copy(dst, src)
 
         def finish(c):
+            width = WIDTHS[c] * GRAIN
             quantise(z_codes[c][:], z_scales[c][:], z_grouped[c][:].rearrange("p v j -> p (v j)"))
-            acc = opsum.tile([P, 2, CHUNK], F32, name="o_acc")
-            for m in range(2):
-                product(acc[:, m, :], w2_codes, w2_scales, slice(m * P, (m + 1) * P), z_codes[c], z_scales[c], slice(0, CHUNK))
-            result = keep.tile([P, 2, CHUNK], F32, name=f"result{c}")
-            nc.scalar.copy(out=result[:], in_=acc[:])
+            result = keep.tile([P, 2, width], F32, name=f"result{c}")
+            if c < CHUNKS - 1:
+                acc = psum.tile([P, 2, width], F32, name="acc")
+                for m in range(2):
+                    product(acc[:, m, :], w2_codes, w2_scales, slice(m * P, (m + 1) * P), z_codes[c], z_scales[c], slice(0, width))
+                nc.scalar.copy(out=result[:], in_=acc[:])
+            else:
+                for m in range(2):
+                    acc = psum.tile([P, width], F32, name="acc")
+                    product(acc[:], w2_codes, w2_scales, slice(m * P, (m + 1) * P), z_codes[c], z_scales[c], slice(0, width))
+                    if m == 0:
+                        nc.scalar.copy(out=result[:, m, :], in_=acc[:])
+                    else:
+                        nc.vector.tensor_copy(result[:, m, :], acc[:])
             nc.sync.dma_start(out_rows[:, :, cells[c]], result[:])
 
         for step in range(CHUNKS + 2):

@@ -17,9 +17,8 @@ P = 128
 PACK = 4
 STRIPE = 16
 HALF = S // 2
-GRAIN = 128
-WIDTHS = (2, 2, 2, 1, 1)
-CHUNKS = len(WIDTHS)
+CHUNK = 256
+CHUNKS = U // CHUNK
 
 
 def tile_picked_unet_none_e_kernel(tc, xT, w1, w2, skip, offs, cell, out):
@@ -31,158 +30,163 @@ def tile_picked_unet_none_e_kernel(tc, xT, w1, w2, skip, offs, cell, out):
         def quantise(codes, scales, grouped):
             nc.vector.quantize_mx(out=codes.bitcast(FP8X4), scales=scales, in_=grouped)
 
+        def product(acc, w_codes, w_scales, codes, scales):
+            nc.tensor.matmul_mx(
+                out=acc,
+                lhsT=w_codes.bitcast(FP8X4),
+                lhsT_scale=w_scales,
+                rhs=codes.bitcast(FP8X4),
+                rhs_scale=scales,
+                start=True,
+                stop=True,
+            )
+
         offs_sb = keep.tile([P, S // STRIPE], U16, name="offs_sb")
         cell_sb = keep.tile([P, S // STRIPE], U16, name="cell_sb")
         x_rows = xT.rearrange("(p j) t -> j p t", j=PACK)
         skip_rows = skip.rearrange("(p j) v -> j p v", j=PACK)
+        w1_rows = w1.rearrange("(p j) c -> p j c", j=PACK)
         x_plane = [keep.tile([P, T], F32, name=f"x_plane{j}") for j in range(PACK)]
-        skip_plane = [keep.tile([P, U], F32, name=f"skip_plane{j}") for j in range(PACK)]
         w1_raw = [keep.tile([P, 2, H], F32, name=f"w1_raw{u}") for u in range(2)]
-        w2_raw = keep.tile([P, PACK, N], F32, name="w2_raw")
+        w2_raw = keep.tile([P, PACK, N], F32, name="w2_raw", tag="late_load")
+        skip_plane = [keep.tile([P, U], F32, name=f"skip_plane{t}") for t in range(PACK - 1)]
 
         nc.sync.dma_start(x_plane[0][:], x_rows[0])
         nc.sync.dma_start(offs_sb[:], offs)
-        w1_rows = w1.rearrange("(p j) c -> p j c", j=PACK)
+        nc.sync.dma_start(cell_sb[:], cell)
         nc.sync.dma_start(w1_raw[0][:], w1_rows[:, 0:2, :])
         for j in range(1, PACK):
             nc.sync.dma_start(x_plane[j][:], x_rows[j])
         nc.sync.dma_start(w1_raw[1][:], w1_rows[:, 2:4, :])
-        nc.sync.dma_start(cell_sb[:], cell)
-        nc.sync.dma_start(skip_plane[0][:], skip_rows[0])
-        nc.sync.dma_start(skip_plane[1][:], skip_rows[1])
+        for t in range(PACK - 1):
+            nc.sync.dma_start(skip_plane[t][:], skip_rows[t])
         nc.sync.dma_start(w2_raw[:], w2.rearrange("(p j) m -> p j m", j=PACK))
-        nc.sync.dma_start(skip_plane[2][:], skip_rows[2])
-        nc.sync.dma_start(skip_plane[3][:], skip_rows[3])
 
         up = [keep.tile([P, U], F32, name=f"up{t}") for t in range(PACK)]
         for t in range(PACK):
             nc.vector.memset(up[t][:], 0.0)
 
-        w1_grouped = [keep.tile([P, P, PACK], BF16, name=f"w1_grouped{t}", align_bytes=64) for t in range(PACK)]
-        w1_codes = [keep.tile([P, P], U32, name=f"w1_codes{t}", align_bytes=64) for t in range(PACK)]
-        w1_scales = [keep.tile([P, P], U8, name=f"w1_scales{t}", align_bytes=64) for t in range(PACK)]
         w1_dealt = [raw[:].rearrange("p e (m t) -> p t m e", t=PACK) for raw in w1_raw]
-        for t in range(PACK):
-            nc.scalar.copy(out=w1_grouped[t][:, :, 0:2], in_=w1_dealt[0][:, t])
+        w1_first = [keep.tile([P, P, PACK], BF16, name=f"w1_first{t}", align_bytes=64) for t in range(2)]
+        for t in range(2):
+            nc.scalar.copy(out=w1_first[t][:, :, 0:2], in_=w1_dealt[0][:, t])
 
         x_grouped = [keep.tile([P, HALF, PACK], BF16, name=f"x_grouped{a}", align_bytes=64) for a in range(2)]
-        x_codes = keep.tile([P, S], U32, name="x_codes", align_bytes=64)
+        x_codes = keep.tile([P, S], U32, name="x_codes", tag="after_x", align_bytes=64)
         x_scales = keep.tile([P, S], U8, name="x_scales", align_bytes=64)
-        list_cols = [slice(a * HALF // STRIPE, (a + 1) * HALF // STRIPE) for a in range(2)]
-        entries = [slice(a * HALF, (a + 1) * HALF) for a in range(2)]
+        halves = [slice(a * HALF, (a + 1) * HALF) for a in range(2)]
+
+        def striped(lst, entries):
+            return lst[:, entries.start // STRIPE : entries.stop // STRIPE]
+
         for j in range(PACK):
             for a in range(2):
-                nc.vector.tensor_copy(x_grouped[a][:, :, j], x_plane[j][:].indirect(offs_sb[:, list_cols[a]]))
+                nc.vector.tensor_copy(x_grouped[a][:, :, j], x_plane[j][:].indirect(striped(offs_sb, halves[a])))
 
-        def quantise_x(a):
-            quantise(x_codes[:, entries[a]], x_scales[:, entries[a]], x_grouped[a][:].rearrange("p s j -> p (s j)"))
-
-        def quantise_w1(t):
-            nc.scalar.copy(out=w1_grouped[t][:, :, 2:4], in_=w1_dealt[1][:, t])
-            quantise(w1_codes[t][:], w1_scales[t][:], w1_grouped[t][:].rearrange("p m j -> p (m j)"))
-
-        quantise_x(0)
-        quantise_w1(0)
-        quantise_x(1)
-        quantise_w1(1)
-
-        def product(acc, w_codes, w_scales, w_cols, codes, scales, cols):
-            nc.tensor.matmul_mx(
-                out=acc,
-                lhsT=w_codes[:, w_cols].bitcast(FP8X4),
-                lhsT_scale=w_scales[:, w_cols],
-                rhs=codes[:, cols].bitcast(FP8X4),
-                rhs_scale=scales[:, cols],
-                start=True,
-                stop=True,
-            )
+        w1_codes = [
+            keep.tile([P, P], U32, name="w1_codes0", tag="relay", align_bytes=64)[:],
+            keep.tile([P, P], U32, name="w1_codes1", align_bytes=64)[:],
+        ]
+        w1_scales = [keep.tile([P, P], U8, name=f"w1_scales{t}", align_bytes=64)[:] for t in range(2)]
+        for a in range(2):
+            quantise(x_codes[:, halves[a]], x_scales[:, halves[a]], x_grouped[a][:].rearrange("p s j -> p (s j)"))
+            nc.scalar.copy(out=w1_first[a][:, :, 2:4], in_=w1_dealt[1][:, a])
+            quantise(w1_codes[a], w1_scales[a], w1_first[a][:].rearrange("p m j -> p (m j)"))
 
         h_sb = [keep.tile([P, S], F32, name=f"h_sb{t}") for t in range(PACK)]
-        pieces = [(0, slice(0, HALF)), (0, slice(HALF, S))] + [(t, slice(0, S)) for t in range(1, PACK)]
-        for n, (t, cols) in enumerate(pieces):
-            if t >= 2:
-                quantise_w1(t)
-            acc = psum.tile([P, S], F32, name="acc")
-            product(acc[:, cols], w1_codes[t], w1_scales[t], slice(0, P), x_codes, x_scales, cols)
-            nc.scalar.copy(out=h_sb[t][:, cols], in_=acc[:, cols])
 
-        w2_grouped = keep.tile([P, N, PACK], BF16, name="w2_grouped", align_bytes=64)
+        def hidden(t, entries):
+            acc = psum.tile([P, S], F32, name="acc")
+            product(acc[:, entries], w1_codes[t], w1_scales[t], x_codes[:, entries], x_scales[:, entries])
+            nc.scalar.copy(out=h_sb[t][:, entries], in_=acc[:, entries])
+
+        def scatter(t, entries):
+            nc.vector.tensor_copy(up[t][:].indirect(striped(cell_sb, entries)), h_sb[t][:, entries])
+
+        for entries in halves:
+            hidden(0, entries)
+            scatter(0, entries)
+
+        w1_rest = keep.tile([P, 2, P, PACK], BF16, name="w1_rest", tag="relay", align_bytes=64)
+        for u in range(2):
+            nc.scalar.copy(
+                out=w1_rest[:, :, :, 2 * u : 2 * u + 2].rearrange("p t m e -> p m e t"),
+                in_=w1_dealt[u][:, 2:4].rearrange("p t m e -> p m e t"),
+            )
+        rest_codes = keep.tile([P, 2 * P], U32, name="rest_codes", align_bytes=64)
+        rest_scales = keep.tile([P, 2 * P], U8, name="rest_scales", align_bytes=64)
+        quantise(rest_codes[:], rest_scales[:], w1_rest[:].rearrange("p t m j -> p (t m j)"))
+        for r in range(2):
+            w1_codes.append(rest_codes[:, r * P : (r + 1) * P])
+            w1_scales.append(rest_scales[:, r * P : (r + 1) * P])
+
+        whole = slice(0, S)
+        z_low = keep.tile([P, 2, U], BF16, name="z_low", tag="relay", align_bytes=64)
+        z_high = [keep.tile([P, 2, U // 2], BF16, name=f"z_high{h}") for h in range(2)]
+        for t in range(1, PACK):
+            hidden(t, whole)
+        for t in range(1, PACK):
+            scatter(t, whole)
+        for t in range(2):
+            nc.gpsimd.tensor_tensor(z_low[:, t, :], up[t][:], skip_plane[t][:], ADD)
+        for h in range(2):
+            part = slice(h * U // 2, (h + 1) * U // 2)
+            nc.gpsimd.tensor_tensor(z_high[h][:, 0, :], up[2][:, part], skip_plane[2][:, part], ADD)
+
+        w2_grouped = keep.tile([P, N, PACK], BF16, name="w2_grouped", tag="after_x", align_bytes=64)
         nc.scalar.copy(
             out=w2_grouped[:].rearrange("p (c i) j -> p c j i", i=4),
             in_=w2_raw[:].rearrange("p j (c i) -> p c j i", i=4),
         )
         w2_codes = keep.tile([P, N], U32, name="w2_codes", align_bytes=64)
         w2_scales = keep.tile([P, N], U8, name="w2_scales", align_bytes=64)
+        quantise(w2_codes[:], w2_scales[:], w2_grouped[:].rearrange("p m j -> p (m j)"))
 
-        grains = U // GRAIN
-        firsts = [sum(WIDTHS[:c]) for c in range(CHUNKS)]
-        spans = [slice(firsts[c], firsts[c] + WIDTHS[c]) for c in range(CHUNKS)]
-        cells = [slice(s.start * GRAIN, s.stop * GRAIN) for s in spans]
-        z_low = keep.tile([P, 2, U], BF16, name="z_low")
-        z_high = keep.tile([P, grains, 2, GRAIN], BF16, name="z_high")
-        z_grouped = [keep.tile([P, WIDTHS[c] * GRAIN, PACK], BF16, name=f"z_grouped{c}", align_bytes=64) for c in range(CHUNKS)]
+        skip_last = keep.tile([P, U], F32, name="skip_last", tag="late_load")
+        nc.sync.dma_start(skip_last[:], skip_rows[PACK - 1])
 
-        def by_grain(ap):
-            return ap.rearrange("p (g v) -> p g v", v=GRAIN)
-
-        def scatter(t, cols):
-            lst = cell_sb[:, cols.start // STRIPE : cols.stop // STRIPE]
-            nc.vector.tensor_copy(up[t][:].indirect(lst), h_sb[t][:, cols])
-
-        for t, cols in pieces:
-            scatter(t, cols)
-            if cols.stop < S:
-                continue
-            if t < 2:
-                nc.gpsimd.tensor_tensor(z_low[:, t, :], up[t][:], skip_plane[t][:], ADD)
-            if t == 1:
-                quantise(w2_codes[:], w2_scales[:], w2_grouped[:].rearrange("p m j -> p (m j)"))
-                for c in range(CHUNKS):
-                    nc.scalar.copy(
-                        out=z_grouped[c][:, :, 0:2],
-                        in_=z_low[:, :, cells[c]].rearrange("p e v -> p v e"),
-                    )
-            if t == 2:
-                nc.gpsimd.tensor_tensor(z_high[:, :, 0, :], by_grain(up[t][:]), by_grain(skip_plane[t][:]), ADD)
-
-        z_codes = [keep.tile([P, WIDTHS[c] * GRAIN], U32, name=f"z_codes{c}", align_bytes=64) for c in range(CHUNKS)]
-        z_scales = [keep.tile([P, WIDTHS[c] * GRAIN], U8, name=f"z_scales{c}", align_bytes=64) for c in range(CHUNKS)]
+        cells = [slice(c * CHUNK, (c + 1) * CHUNK) for c in range(CHUNKS)]
+        z_grouped = [keep.tile([P, CHUNK, PACK], BF16, name=f"z_grouped{c}", align_bytes=64) for c in range(CHUNKS)]
+        for c in range(CHUNKS):
+            nc.scalar.copy(out=z_grouped[c][:, :, 0:2], in_=z_low[:, :, cells[c]].rearrange("p e v -> p v e"))
         out_rows = out.rearrange("(m p) v -> p m v", p=P)
 
+        def high(c):
+            return z_high[c // 2][:, :, cells[c % 2]]
+
         def add_last(c):
-            nc.vector.tensor_tensor(z_high[:, spans[c], 1, :], by_grain(up[3][:, cells[c]]), by_grain(skip_plane[3][:, cells[c]]), ADD)
+            nc.vector.tensor_tensor(high(c)[:, 1, :], up[PACK - 1][:, cells[c]], skip_last[:, cells[c]], ADD)
 
-        def weave(c):
-            dst = z_grouped[c][:, :, 2:4].rearrange("p (g v) e -> p g v e", v=GRAIN)
-            src = z_high[:, spans[c], :, :].rearrange("p g e v -> p g v e")
-            if c == 1:
-                nc.scalar.copy(out=dst, in_=src)
-            else:
-                nc.vector.tensor_copy(dst, src)
+        def weave(c, copy):
+            copy(z_grouped[c][:, :, 2:4], high(c).rearrange("p e v -> p v e"))
 
-        def finish(c):
-            width = WIDTHS[c] * GRAIN
-            quantise(z_codes[c][:], z_scales[c][:], z_grouped[c][:].rearrange("p v j -> p (v j)"))
-            result = keep.tile([P, 2, width], F32, name=f"result{c}")
-            if c < CHUNKS - 1:
-                acc = psum.tile([P, 2, width], F32, name="acc")
-                for m in range(2):
-                    product(acc[:, m, :], w2_codes, w2_scales, slice(m * P, (m + 1) * P), z_codes[c], z_scales[c], slice(0, width))
-                nc.scalar.copy(out=result[:], in_=acc[:])
-            else:
-                for m in range(2):
-                    acc = psum.tile([P, width], F32, name="acc")
-                    product(acc[:], w2_codes, w2_scales, slice(m * P, (m + 1) * P), z_codes[c], z_scales[c], slice(0, width))
-                    if m == 0:
-                        nc.scalar.copy(out=result[:, m, :], in_=acc[:])
-                    else:
-                        nc.vector.tensor_copy(result[:, m, :], acc[:])
-            nc.sync.dma_start(out_rows[:, :, cells[c]], result[:])
+        def finish(c, part, copies):
+            width = part.stop - part.start
+            first = cells[c].start + part.start
+            codes = keep.tile([P, width], U32, name=f"z_codes{first}", align_bytes=64)
+            scales = keep.tile([P, width], U8, name=f"z_scales{first}", align_bytes=64)
+            quantise(codes[:], scales[:], z_grouped[c][:, part, :].rearrange("p v j -> p (v j)"))
+            result = keep.tile([P, 2, width], F32, name=f"result{first}")
+            share = 2 // len(copies)
+            for n, copy in enumerate(copies):
+                acc = psum.tile([P, share, width], F32, name="acc")
+                for r in range(share):
+                    rows = slice((n * share + r) * P, (n * share + r + 1) * P)
+                    product(acc[:, r, :], w2_codes[:, rows], w2_scales[:, rows], codes[:], scales[:])
+                copy(result[:, n * share : (n + 1) * share, :], acc[:])
+            nc.sync.dma_start(out_rows[:, :, first : first + width], result[:])
 
-        for step in range(CHUNKS + 2):
-            if step < CHUNKS:
-                add_last(step)
-            if 1 <= step <= CHUNKS:
-                weave(step - 1)
-            if step >= 2:
-                finish(step - 2)
+        on_scalar, on_vector = nc.scalar.copy, nc.vector.tensor_copy
+        add_last(0)
+        add_last(1)
+        weave(0, on_vector)
+        weave(1, on_scalar)
+        add_last(2)
+        weave(2, on_scalar)
+        finish(0, slice(0, CHUNK), [on_scalar])
+        add_last(3)
+        finish(1, slice(0, CHUNK), [on_scalar])
+        weave(3, on_vector)
+        finish(2, slice(0, CHUNK), [on_scalar])
+        finish(3, slice(0, CHUNK // 2), [on_vector])
+        finish(3, slice(CHUNK // 2, CHUNK), [on_scalar, on_vector])

@@ -1,6 +1,7 @@
 from contextlib import ExitStack
 
 import concourse.mybir as mybir
+from concourse.masks import make_identity
 
 K, T, S, H, N, U = 512, 2048, 512, 512, 256, 1024
 FLOPS = 2 * K * H * S + 2 * H * N * U
@@ -25,7 +26,10 @@ def tile_picked_unet_none_e_kernel(tc, xT, w1, w2, skip, offs, cell, out):
     nc = tc.nc
     with ExitStack() as ctx:
         keep = ctx.enter_context(tc.tile_pool(name="keep", bufs=1))
-        psum = ctx.enter_context(tc.psum_pool(name="psum", bufs=8))
+        psum = ctx.enter_context(tc.psum_pool(name="psum", bufs=1))
+
+        def bank(b, shape):
+            return psum.tile([P, *shape], F32, name="bank", tag=f"bank{b}")
 
         def quantise(codes, scales, grouped):
             nc.vector.quantize_mx(out=codes.bitcast(FP8X4), scales=scales, in_=grouped)
@@ -65,6 +69,12 @@ def tile_picked_unet_none_e_kernel(tc, xT, w1, w2, skip, offs, cell, out):
         up = [keep.tile([P, U], F32, name=f"up{t}") for t in range(PACK)]
         for t in range(PACK):
             nc.vector.memset(up[t][:], 0.0)
+        identity = keep.tile([P, P], F32, name="identity")
+        make_identity(nc, identity[:])
+        turned_low = [keep.tile([P, 2, P, 2], BF16, name=f"turned_low{c}") for c in range(CHUNKS)]
+        turned_third = {c: keep.tile([P, 2, P, 2], BF16, name=f"turned_third{c}", tag=f"third{c}") for c in (3, 2)}
+        for c in (3, 2):
+            nc.vector.memset(turned_third[c][:], 0.0)
 
         w1_dealt = [raw[:].rearrange("p e (m t) -> p t m e", t=PACK) for raw in w1_raw]
         w1_first = [keep.tile([P, P, PACK], BF16, name=f"w1_first{t}", align_bytes=64) for t in range(2)]
@@ -88,24 +98,37 @@ def tile_picked_unet_none_e_kernel(tc, xT, w1, w2, skip, offs, cell, out):
             keep.tile([P, P], U32, name="w1_codes1", align_bytes=64)[:],
         ]
         w1_scales = [keep.tile([P, P], U8, name=f"w1_scales{t}", align_bytes=64)[:] for t in range(2)]
-        for a in range(2):
-            quantise(x_codes[:, halves[a]], x_scales[:, halves[a]], x_grouped[a][:].rearrange("p s j -> p (s j)"))
-            nc.scalar.copy(out=w1_first[a][:, :, 2:4], in_=w1_dealt[1][:, a])
-            quantise(w1_codes[a], w1_scales[a], w1_first[a][:].rearrange("p m j -> p (m j)"))
+        pieces = [slice(0, P), slice(P, HALF), slice(HALF, S)]
 
-        h_sb = [keep.tile([P, S], F32, name=f"h_sb{t}") for t in range(PACK)]
+        def quantise_x(entries):
+            a = entries.start // HALF
+            part = x_grouped[a][:, entries.start - a * HALF : entries.stop - a * HALF, :]
+            quantise(x_codes[:, entries], x_scales[:, entries], part.rearrange("p s j -> p (s j)"))
 
-        def hidden(t, entries):
-            acc = psum.tile([P, S], F32, name="acc")
+        def quantise_w1(t):
+            nc.scalar.copy(out=w1_first[t][:, :, 2:4], in_=w1_dealt[1][:, t])
+            quantise(w1_codes[t], w1_scales[t], w1_first[t][:].rearrange("p m j -> p (m j)"))
+
+        quantise_x(pieces[0])
+        quantise_w1(0)
+        quantise_x(pieces[1])
+        quantise_x(pieces[2])
+        quantise_w1(1)
+
+
+        def hidden(t, entries, b):
+            acc = bank(b, [S])
             product(acc[:, entries], w1_codes[t], w1_scales[t], x_codes[:, entries], x_scales[:, entries])
-            nc.scalar.copy(out=h_sb[t][:, entries], in_=acc[:, entries])
+            width = entries.stop - entries.start
+            h_sb = keep.tile([P, width], F32, name="h_sb", tag=f"h{t}_{entries.start}", align_bytes=64)
+            nc.scalar.copy(out=h_sb[:], in_=acc[:, entries])
+            return h_sb
 
-        def scatter(t, entries):
-            nc.vector.tensor_copy(up[t][:].indirect(striped(cell_sb, entries)), h_sb[t][:, entries])
+        def scatter(t, entries, h_sb):
+            nc.vector.tensor_copy(up[t][:].indirect(striped(cell_sb, entries)), h_sb[:])
 
-        for entries in halves:
-            hidden(0, entries)
-            scatter(0, entries)
+        for n, entries in enumerate(pieces):
+            scatter(0, entries, hidden(0, entries, 5 + n))
 
         w1_rest = keep.tile([P, 2, P, PACK], BF16, name="w1_rest", tag="relay", align_bytes=64)
         for u in range(2):
@@ -113,7 +136,7 @@ def tile_picked_unet_none_e_kernel(tc, xT, w1, w2, skip, offs, cell, out):
                 out=w1_rest[:, :, :, 2 * u : 2 * u + 2].rearrange("p t m e -> p m e t"),
                 in_=w1_dealt[u][:, 2:4].rearrange("p t m e -> p m e t"),
             )
-        rest_codes = keep.tile([P, 2 * P], U32, name="rest_codes", align_bytes=64)
+        rest_codes = keep.tile([P, 2 * P], U32, name="rest_codes", tag=f"h0_{HALF}", align_bytes=64)
         rest_scales = keep.tile([P, 2 * P], U8, name="rest_scales", align_bytes=64)
         quantise(rest_codes[:], rest_scales[:], w1_rest[:].rearrange("p t m j -> p (t m j)"))
         for r in range(2):
@@ -121,17 +144,8 @@ def tile_picked_unet_none_e_kernel(tc, xT, w1, w2, skip, offs, cell, out):
             w1_scales.append(rest_scales[:, r * P : (r + 1) * P])
 
         whole = slice(0, S)
-        z_low = keep.tile([P, 2, U], BF16, name="z_low", tag="relay", align_bytes=64)
-        z_high = [keep.tile([P, 2, U // 2], BF16, name=f"z_high{h}") for h in range(2)]
         for t in range(1, PACK):
-            hidden(t, whole)
-        for t in range(1, PACK):
-            scatter(t, whole)
-        for t in range(2):
-            nc.gpsimd.tensor_tensor(z_low[:, t, :], up[t][:], skip_plane[t][:], ADD)
-        for h in range(2):
-            part = slice(h * U // 2, (h + 1) * U // 2)
-            nc.gpsimd.tensor_tensor(z_high[h][:, 0, :], up[2][:, part], skip_plane[2][:, part], ADD)
+            scatter(t, whole, hidden(t, whole, 4 + t))
 
         w2_grouped = keep.tile([P, N, PACK], BF16, name="w2_grouped", tag="after_x", align_bytes=64)
         nc.scalar.copy(
@@ -147,46 +161,91 @@ def tile_picked_unet_none_e_kernel(tc, xT, w1, w2, skip, offs, cell, out):
 
         cells = [slice(c * CHUNK, (c + 1) * CHUNK) for c in range(CHUNKS)]
         z_grouped = [keep.tile([P, CHUNK, PACK], BF16, name=f"z_grouped{c}", align_bytes=64) for c in range(CHUNKS)]
-        for c in range(CHUNKS):
-            nc.scalar.copy(out=z_grouped[c][:, :, 0:2], in_=z_low[:, :, cells[c]].rearrange("p e v -> p v e"))
-        out_rows = out.rearrange("(m p) v -> p m v", p=P)
 
-        def high(c):
-            return z_high[c // 2][:, :, cells[c % 2]]
+        def turn(dst, src, start, stop):
+            nc.tensor.matmul(dst, lhsT=src, rhs=identity[:], start=start, stop=stop, is_transpose=True)
+
+        def block(tile, n):
+            return tile[:, n * P : (n + 1) * P]
+
+        low_sums = [bank(c, [2, 2, P]) for c in range(CHUNKS)]
+        for t in range(2):
+            for c in range(CHUNKS):
+                for g in range(2):
+                    turn(low_sums[c][:, g, t, :], block(skip_plane[t], 2 * c + g), t == 0 and g == 0, False)
+        for t in range(2):
+            for c in range(CHUNKS):
+                for g in range(2):
+                    turn(low_sums[c][:, g, t, :], block(up[t], 2 * c + g), False, t == 1 and g == 1)
+        pairs = []
+        for c in range(CHUNKS):
+            nc.scalar.copy(out=turned_low[c][:], in_=low_sums[c][:].rearrange("v g e p -> v g p e"))
+            pairs.append(bank(CHUNKS if c == 2 else c, [2, CHUNK]))
+
+        def turn_back(u, c, blocks):
+            words = blocks.rearrange("v g p e -> v (g p e)").bitcast(F32)
+            for g in range(2):
+                turn(pairs[c][:, u, g * P : (g + 1) * P], block(words, g), True, True)
+
+        for c in range(CHUNKS):
+            turn_back(0, c, turned_low[c][:])
+
+        def words_of(c):
+            return z_grouped[c][:].rearrange("p v j -> p (v j)").bitcast(F32).rearrange("p (v u) -> p v u", u=2)
+
+        for c in range(2):
+            nc.scalar.copy(out=words_of(c)[:, :, 0], in_=pairs[c][:, 0, :])
+        third_sums = bank(2, [4, P])
+        for n in range(4):
+            turn(third_sums[:, n, :], block(skip_plane[2], 4 + n), n == 0, False)
+        for n in range(4):
+            turn(third_sums[:, n, :], block(up[2], 4 + n), False, n == 3)
+        for c in (3, 2):
+            nc.scalar.copy(out=turned_third[c][:, :, :, 0], in_=third_sums[:, 2 * (c - 2) : 2 * (c - 2) + 2, :])
+        for c in (3, 2):
+            turn_back(1, c, turned_third[c][:])
+        for c in (3, 2):
+            nc.scalar.copy(out=words_of(c), in_=pairs[c][:].rearrange("p u v -> p v u"))
+
+        out_rows = out.rearrange("(m p) v -> p m v", p=P)
+        z_high = keep.tile([P, 2, U // 2], BF16, name="z_high", tag="third3")
+        z_rest = keep.tile([P, U // 2], BF16, name="z_rest", tag="third2")
+        z_last = [z_high[:, 1, cells[0]], z_high[:, 1, cells[1]], z_rest[:, cells[0]], z_rest[:, cells[1]]]
 
         def add_last(c):
-            nc.vector.tensor_tensor(high(c)[:, 1, :], up[PACK - 1][:, cells[c]], skip_last[:, cells[c]], ADD)
+            nc.vector.tensor_tensor(z_last[c], up[PACK - 1][:, cells[c]], skip_last[:, cells[c]], ADD)
 
         def weave(c, copy):
-            copy(z_grouped[c][:, :, 2:4], high(c).rearrange("p e v -> p v e"))
+            if c < 2:
+                copy(z_grouped[c][:, :, 2:4], z_high[:, :, cells[c]].rearrange("p e v -> p v e"))
+            else:
+                copy(z_grouped[c][:, :, PACK - 1], z_last[c])
 
-        def finish(c, part, copies):
+        def finish(c, part, copy, b):
             width = part.stop - part.start
             first = cells[c].start + part.start
             codes = keep.tile([P, width], U32, name=f"z_codes{first}", align_bytes=64)
             scales = keep.tile([P, width], U8, name=f"z_scales{first}", align_bytes=64)
             quantise(codes[:], scales[:], z_grouped[c][:, part, :].rearrange("p v j -> p (v j)"))
             result = keep.tile([P, 2, width], F32, name=f"result{first}")
-            share = 2 // len(copies)
-            for n, copy in enumerate(copies):
-                acc = psum.tile([P, share, width], F32, name="acc")
-                for r in range(share):
-                    rows = slice((n * share + r) * P, (n * share + r + 1) * P)
-                    product(acc[:, r, :], w2_codes[:, rows], w2_scales[:, rows], codes[:], scales[:])
-                copy(result[:, n * share : (n + 1) * share, :], acc[:])
+            acc = bank(b, [2, width])
+            for m in range(2):
+                product(acc[:, m, :], block(w2_codes, m), block(w2_scales, m), codes[:], scales[:])
+            copy(result[:], acc[:])
             nc.sync.dma_start(out_rows[:, :, first : first + width], result[:])
 
         on_scalar, on_vector = nc.scalar.copy, nc.vector.tensor_copy
+        nc.vector.tensor_tensor(z_high[:, 0, :], up[2][:, 0 : U // 2], skip_plane[2][:, 0 : U // 2], ADD)
         add_last(0)
-        add_last(1)
-        weave(0, on_vector)
-        weave(1, on_scalar)
         add_last(2)
+        weave(0, on_vector)
         weave(2, on_scalar)
-        finish(0, slice(0, CHUNK), [on_scalar])
         add_last(3)
-        finish(1, slice(0, CHUNK), [on_scalar])
-        weave(3, on_vector)
-        finish(2, slice(0, CHUNK), [on_scalar])
-        finish(3, slice(0, CHUNK // 2), [on_vector])
-        finish(3, slice(CHUNK // 2, CHUNK), [on_scalar, on_vector])
+        weave(3, on_scalar)
+        finish(0, slice(0, CHUNK), on_scalar, 5)
+        add_last(1)
+        finish(2, slice(0, CHUNK), on_scalar, 6)
+        weave(1, on_vector)
+        finish(3, slice(0, CHUNK), on_scalar, 7)
+        finish(1, slice(0, CHUNK // 2), on_vector, 2)
+        finish(1, slice(CHUNK // 2, CHUNK), on_vector, 0)

@@ -20,6 +20,12 @@ STRIPE = 16
 HALF = S // 2
 CHUNK = 256
 CHUNKS = U // CHUNK
+BLOCKS = CHUNK // P
+LAST = PACK - 1
+VECTOR_CHUNKS = (0, 1)
+TENSOR_CHUNKS = (3, 2)
+SPARE_BANK = CHUNKS
+FIRST_H_BANK = CHUNKS + 1
 
 
 def tile_picked_unet_none_e_kernel(tc, xT, w1, w2, skip, offs, cell, out):
@@ -49,21 +55,21 @@ def tile_picked_unet_none_e_kernel(tc, xT, w1, w2, skip, offs, cell, out):
         cell_sb = keep.tile([P, S // STRIPE], U16, name="cell_sb")
         x_rows = xT.rearrange("(p j) t -> j p t", j=PACK)
         skip_rows = skip.rearrange("(p j) v -> j p v", j=PACK)
-        w1_rows = w1.rearrange("(p j) c -> p j c", j=PACK)
+        w1_halves = w1.rearrange("(p j) (h c) -> h p j c", j=PACK, h=2)
         x_plane = [keep.tile([P, T], F32, name=f"x_plane{j}") for j in range(PACK)]
-        w1_raw = [keep.tile([P, 2, H], F32, name=f"w1_raw{u}") for u in range(2)]
+        w1_raw = [keep.tile([P, PACK, H // 2], F32, name=f"w1_raw{h}") for h in range(2)]
         w2_raw = keep.tile([P, PACK, N], F32, name="w2_raw", tag="late_load")
-        skip_plane = [keep.tile([P, U], F32, name=f"skip_plane{t}") for t in range(PACK - 1)]
+        skip_plane = [keep.tile([P, U], F32, name=f"skip_plane{j}") for j in range(LAST)]
 
         nc.sync.dma_start(x_plane[0][:], x_rows[0])
         nc.sync.dma_start(offs_sb[:], offs)
         nc.sync.dma_start(cell_sb[:], cell)
-        nc.sync.dma_start(w1_raw[0][:], w1_rows[:, 0:2, :])
+        nc.sync.dma_start(w1_raw[0][:], w1_halves[0])
         for j in range(1, PACK):
             nc.sync.dma_start(x_plane[j][:], x_rows[j])
-        nc.sync.dma_start(w1_raw[1][:], w1_rows[:, 2:4, :])
-        for t in range(PACK - 1):
-            nc.sync.dma_start(skip_plane[t][:], skip_rows[t])
+        nc.sync.dma_start(w1_raw[1][:], w1_halves[1])
+        for j in range(LAST):
+            nc.sync.dma_start(skip_plane[j][:], skip_rows[j])
         nc.sync.dma_start(w2_raw[:], w2.rearrange("(p j) m -> p j m", j=PACK))
 
         up = [keep.tile([P, U], F32, name=f"up{t}") for t in range(PACK)]
@@ -71,93 +77,72 @@ def tile_picked_unet_none_e_kernel(tc, xT, w1, w2, skip, offs, cell, out):
             nc.vector.memset(up[t][:], 0.0)
         identity = keep.tile([P, P], F32, name="identity")
         make_identity(nc, identity[:])
-        turned_low = [keep.tile([P, 2, P, 2], BF16, name=f"turned_low{c}") for c in range(CHUNKS)]
-        turned_third = {c: keep.tile([P, 2, P, 2], BF16, name=f"turned_third{c}", tag=f"third{c}") for c in (3, 2)}
-        for c in (3, 2):
+        turned_low = [keep.tile([P, BLOCKS, P, 2], BF16, name=f"turned_low{c}") for c in range(CHUNKS)]
+        turned_third = {
+            c: keep.tile([P, BLOCKS, P, 2], BF16, name=f"turned_third{c}", tag=f"third{c}") for c in TENSOR_CHUNKS
+        }
+        for c in TENSOR_CHUNKS:
             nc.vector.memset(turned_third[c][:], 0.0)
 
-        w1_dealt = [raw[:].rearrange("p e (m t) -> p t m e", t=PACK) for raw in w1_raw]
-        w1_first = [keep.tile([P, P, PACK], BF16, name=f"w1_first{t}", align_bytes=64) for t in range(2)]
-        for t in range(2):
-            nc.scalar.copy(out=w1_first[t][:, :, 0:2], in_=w1_dealt[0][:, t])
+        w1_low = [keep.tile([P, 2, P // 2, PACK], BF16, name=f"w1_low{h}", align_bytes=64) for h in range(2)]
+        w1_high = keep.tile([P, 2, 2, P // 2, PACK], BF16, name="w1_high", align_bytes=64)
+        w1_codes = keep.tile([P, H], U32, name="w1_codes", align_bytes=64)
+        w1_scales = keep.tile([P, H], U8, name="w1_scales", align_bytes=64)
+
+        def block(tile, n):
+            return tile[:, n * P : (n + 1) * P]
+
+        def deal_w1(h):
+            dealt = w1_raw[h][:].rearrange("p j (r t) -> p r j t", t=PACK)
+            nc.scalar.copy(out=w1_low[h][:].rearrange("p e r j -> p r j e"), in_=dealt[:, :, :, 0:2])
+            nc.scalar.copy(out=w1_high[:, :, h].rearrange("p e r j -> p r j e"), in_=dealt[:, :, :, 2:4])
+            quantise(block(w1_codes, h), block(w1_scales, h), w1_low[h][:].rearrange("p e r j -> p (e r j)"))
+
+        deal_w1(0)
 
         x_grouped = [keep.tile([P, HALF, PACK], BF16, name=f"x_grouped{a}", align_bytes=64) for a in range(2)]
         x_codes = keep.tile([P, S], U32, name="x_codes", tag="after_x", align_bytes=64)
         x_scales = keep.tile([P, S], U8, name="x_scales", align_bytes=64)
         halves = [slice(a * HALF, (a + 1) * HALF) for a in range(2)]
 
-        def striped(lst, entries):
-            return lst[:, entries.start // STRIPE : entries.stop // STRIPE]
+        def striped(list_sb, entries):
+            return list_sb[:, entries.start // STRIPE : entries.stop // STRIPE]
 
         for j in range(PACK):
             for a in range(2):
                 nc.vector.tensor_copy(x_grouped[a][:, :, j], x_plane[j][:].indirect(striped(offs_sb, halves[a])))
 
-        w1_codes = [
-            keep.tile([P, P], U32, name="w1_codes0", tag="relay", align_bytes=64)[:],
-            keep.tile([P, P], U32, name="w1_codes1", align_bytes=64)[:],
-        ]
-        w1_scales = [keep.tile([P, P], U8, name=f"w1_scales{t}", align_bytes=64)[:] for t in range(2)]
         pieces = [slice(0, P), slice(P, HALF), slice(HALF, S)]
-
-        def quantise_x(entries):
+        for entries in pieces:
             a = entries.start // HALF
-            part = x_grouped[a][:, entries.start - a * HALF : entries.stop - a * HALF, :]
-            quantise(x_codes[:, entries], x_scales[:, entries], part.rearrange("p s j -> p (s j)"))
+            grouped = x_grouped[a][:, entries.start - a * HALF : entries.stop - a * HALF, :]
+            quantise(x_codes[:, entries], x_scales[:, entries], grouped.rearrange("p s j -> p (s j)"))
+        deal_w1(1)
+        quantise(w1_codes[:, 2 * P :], w1_scales[:, 2 * P :], w1_high[:].rearrange("p e h r j -> p (e h r j)"))
 
-        def quantise_w1(t):
-            nc.scalar.copy(out=w1_first[t][:, :, 2:4], in_=w1_dealt[1][:, t])
-            quantise(w1_codes[t], w1_scales[t], w1_first[t][:].rearrange("p m j -> p (m j)"))
-
-        quantise_x(pieces[0])
-        quantise_w1(0)
-        quantise_x(pieces[1])
-        quantise_x(pieces[2])
-        quantise_w1(1)
-
-
-        def hidden(t, entries, b):
+        def put(t, entries, b):
             acc = bank(b, [S])
-            product(acc[:, entries], w1_codes[t], w1_scales[t], x_codes[:, entries], x_scales[:, entries])
-            width = entries.stop - entries.start
-            h_sb = keep.tile([P, width], F32, name="h_sb", tag=f"h{t}_{entries.start}", align_bytes=64)
+            product(acc[:, entries], block(w1_codes, t), block(w1_scales, t), x_codes[:, entries], x_scales[:, entries])
+            h_sb = keep.tile([P, entries.stop - entries.start], F32, name=f"h{t}_{entries.start}")
             nc.scalar.copy(out=h_sb[:], in_=acc[:, entries])
-            return h_sb
-
-        def scatter(t, entries, h_sb):
             nc.vector.tensor_copy(up[t][:].indirect(striped(cell_sb, entries)), h_sb[:])
 
         for n, entries in enumerate(pieces):
-            scatter(0, entries, hidden(0, entries, 5 + n))
-
-        w1_rest = keep.tile([P, 2, P, PACK], BF16, name="w1_rest", tag="relay", align_bytes=64)
-        for u in range(2):
-            nc.scalar.copy(
-                out=w1_rest[:, :, :, 2 * u : 2 * u + 2].rearrange("p t m e -> p m e t"),
-                in_=w1_dealt[u][:, 2:4].rearrange("p t m e -> p m e t"),
-            )
-        rest_codes = keep.tile([P, 2 * P], U32, name="rest_codes", tag=f"h0_{HALF}", align_bytes=64)
-        rest_scales = keep.tile([P, 2 * P], U8, name="rest_scales", align_bytes=64)
-        quantise(rest_codes[:], rest_scales[:], w1_rest[:].rearrange("p t m j -> p (t m j)"))
-        for r in range(2):
-            w1_codes.append(rest_codes[:, r * P : (r + 1) * P])
-            w1_scales.append(rest_scales[:, r * P : (r + 1) * P])
-
-        whole = slice(0, S)
+            put(0, entries, FIRST_H_BANK + n)
         for t in range(1, PACK):
-            scatter(t, whole, hidden(t, whole, 4 + t))
+            put(t, slice(0, S), FIRST_H_BANK + t - 1)
 
         w2_grouped = keep.tile([P, N, PACK], BF16, name="w2_grouped", tag="after_x", align_bytes=64)
         nc.scalar.copy(
-            out=w2_grouped[:].rearrange("p (c i) j -> p c j i", i=4),
-            in_=w2_raw[:].rearrange("p j (c i) -> p c j i", i=4),
+            out=w2_grouped[:].rearrange("p (c i) j -> p c j i", i=PACK),
+            in_=w2_raw[:].rearrange("p j (c i) -> p c j i", i=PACK),
         )
         w2_codes = keep.tile([P, N], U32, name="w2_codes", align_bytes=64)
         w2_scales = keep.tile([P, N], U8, name="w2_scales", align_bytes=64)
         quantise(w2_codes[:], w2_scales[:], w2_grouped[:].rearrange("p m j -> p (m j)"))
 
         skip_last = keep.tile([P, U], F32, name="skip_last", tag="late_load")
-        nc.sync.dma_start(skip_last[:], skip_rows[PACK - 1])
+        nc.sync.dma_start(skip_last[:], skip_rows[LAST])
 
         cells = [slice(c * CHUNK, (c + 1) * CHUNK) for c in range(CHUNKS)]
         z_grouped = [keep.tile([P, CHUNK, PACK], BF16, name=f"z_grouped{c}", align_bytes=64) for c in range(CHUNKS)]
@@ -165,61 +150,71 @@ def tile_picked_unet_none_e_kernel(tc, xT, w1, w2, skip, offs, cell, out):
         def turn(dst, src, start, stop):
             nc.tensor.matmul(dst, lhsT=src, rhs=identity[:], start=start, stop=stop, is_transpose=True)
 
-        def block(tile, n):
-            return tile[:, n * P : (n + 1) * P]
+        low_sums = [bank(c, [BLOCKS, 2, 2, P // 2]) for c in range(CHUNKS)]
+        for e in range(2):
+            for c in range(CHUNKS):
+                for g in range(BLOCKS):
+                    turn(low_sums[c][:, g, :, e, :], block(skip_plane[e], BLOCKS * c + g), e == 0 and g == 0, False)
+        for h in range(2):
+            for c in range(CHUNKS):
+                for g in range(BLOCKS):
+                    columns = low_sums[c][:, g, h].rearrange("v e r -> v (e r)")
+                    turn(columns, block(up[h], BLOCKS * c + g), False, h == 1 and g == BLOCKS - 1)
 
-        low_sums = [bank(c, [2, 2, P]) for c in range(CHUNKS)]
-        for t in range(2):
-            for c in range(CHUNKS):
-                for g in range(2):
-                    turn(low_sums[c][:, g, t, :], block(skip_plane[t], 2 * c + g), t == 0 and g == 0, False)
-        for t in range(2):
-            for c in range(CHUNKS):
-                for g in range(2):
-                    turn(low_sums[c][:, g, t, :], block(up[t], 2 * c + g), False, t == 1 and g == 1)
+        third_bank = CHUNKS - 2
         pairs = []
         for c in range(CHUNKS):
-            nc.scalar.copy(out=turned_low[c][:], in_=low_sums[c][:].rearrange("v g e p -> v g p e"))
-            pairs.append(bank(CHUNKS if c == 2 else c, [2, CHUNK]))
+            nc.scalar.copy(
+                out=turned_low[c][:].rearrange("v g (h r) e -> v (g h) r e", h=2),
+                in_=low_sums[c][:].rearrange("v g h e r -> v (g h) r e"),
+            )
+            pairs.append(bank(SPARE_BANK if c == third_bank else c, [2, CHUNK]))
 
-        def turn_back(u, c, blocks):
-            words = blocks.rearrange("v g p e -> v (g p e)").bitcast(F32)
-            for g in range(2):
+        def turn_back(u, c, turned):
+            words = turned[:].rearrange("v g p e -> v (g p e)").bitcast(F32)
+            for g in range(BLOCKS):
                 turn(pairs[c][:, u, g * P : (g + 1) * P], block(words, g), True, True)
 
         for c in range(CHUNKS):
-            turn_back(0, c, turned_low[c][:])
+            turn_back(0, c, turned_low[c])
 
-        def words_of(c):
+        def z_words(c):
             return z_grouped[c][:].rearrange("p v j -> p (v j)").bitcast(F32).rearrange("p (v u) -> p v u", u=2)
 
-        for c in range(2):
-            nc.scalar.copy(out=words_of(c)[:, :, 0], in_=pairs[c][:, 0, :])
-        third_sums = bank(2, [4, P])
-        for n in range(4):
-            turn(third_sums[:, n, :], block(skip_plane[2], 4 + n), n == 0, False)
-        for n in range(4):
-            turn(third_sums[:, n, :], block(up[2], 4 + n), False, n == 3)
-        for c in (3, 2):
-            nc.scalar.copy(out=turned_third[c][:, :, :, 0], in_=third_sums[:, 2 * (c - 2) : 2 * (c - 2) + 2, :])
-        for c in (3, 2):
-            turn_back(1, c, turned_third[c][:])
-        for c in (3, 2):
-            nc.scalar.copy(out=words_of(c), in_=pairs[c][:].rearrange("p u v -> p v u"))
+        for c in VECTOR_CHUNKS:
+            nc.scalar.copy(out=z_words(c)[:, :, 0], in_=pairs[c][:, 0, :])
+
+        upper = min(TENSOR_CHUNKS)
+        third_blocks = BLOCKS * len(TENSOR_CHUNKS)
+        third_sums = bank(third_bank, [third_blocks, P])
+        for n in range(third_blocks):
+            turn(third_sums[:, n, :], block(skip_plane[2], BLOCKS * upper + n), n == 0, False)
+        for n in range(third_blocks):
+            turn(third_sums[:, n, :], block(up[2], BLOCKS * upper + n), False, n == third_blocks - 1)
+        for c in TENSOR_CHUNKS:
+            own = slice(BLOCKS * (c - upper), BLOCKS * (c - upper + 1))
+            nc.scalar.copy(out=turned_third[c][:, :, :, 0], in_=third_sums[:, own, :])
+        for c in TENSOR_CHUNKS:
+            turn_back(1, c, turned_third[c])
+        for c in TENSOR_CHUNKS:
+            nc.scalar.copy(out=z_words(c), in_=pairs[c][:].rearrange("p u v -> p v u"))
 
         out_rows = out.rearrange("(m p) v -> p m v", p=P)
-        z_high = keep.tile([P, 2, U // 2], BF16, name="z_high", tag="third3")
-        z_rest = keep.tile([P, U // 2], BF16, name="z_rest", tag="third2")
-        z_last = [z_high[:, 1, cells[0]], z_high[:, 1, cells[1]], z_rest[:, cells[0]], z_rest[:, cells[1]]]
+        z_lower = keep.tile([P, 2, U // 2], BF16, name="z_lower", tag=f"third{TENSOR_CHUNKS[0]}")
+        z_upper = keep.tile([P, U // 2], BF16, name="z_upper", tag=f"third{TENSOR_CHUNKS[1]}")
+
+        def add_third(c):
+            nc.vector.tensor_tensor(z_lower[:, 0, cells[c]], up[2][:, cells[c]], skip_plane[2][:, cells[c]], ADD)
 
         def add_last(c):
-            nc.vector.tensor_tensor(z_last[c], up[PACK - 1][:, cells[c]], skip_last[:, cells[c]], ADD)
+            sums = z_lower[:, 1, cells[c]] if c in VECTOR_CHUNKS else z_upper[:, cells[c - upper]]
+            nc.vector.tensor_tensor(sums, up[LAST][:, cells[c]], skip_last[:, cells[c]], ADD)
 
-        def weave(c, copy):
-            if c < 2:
-                copy(z_grouped[c][:, :, 2:4], z_high[:, :, cells[c]].rearrange("p e v -> p v e"))
-            else:
-                copy(z_grouped[c][:, :, PACK - 1], z_last[c])
+        def weave_lower(c):
+            nc.vector.tensor_copy(z_grouped[c][:, :, 2:4], z_lower[:, :, cells[c]].rearrange("p e v -> p v e"))
+
+        def weave_upper(c):
+            nc.scalar.copy(out=z_grouped[c][:, :, LAST], in_=z_upper[:, cells[c - upper]])
 
         def finish(c, part, copy, b):
             width = part.stop - part.start
@@ -227,25 +222,26 @@ def tile_picked_unet_none_e_kernel(tc, xT, w1, w2, skip, offs, cell, out):
             codes = keep.tile([P, width], U32, name=f"z_codes{first}", align_bytes=64)
             scales = keep.tile([P, width], U8, name=f"z_scales{first}", align_bytes=64)
             quantise(codes[:], scales[:], z_grouped[c][:, part, :].rearrange("p v j -> p (v j)"))
-            result = keep.tile([P, 2, width], F32, name=f"result{first}")
-            acc = bank(b, [2, width])
-            for m in range(2):
+            result = keep.tile([P, N // P, width], F32, name=f"result{first}")
+            acc = bank(b, [N // P, width])
+            for m in range(N // P):
                 product(acc[:, m, :], block(w2_codes, m), block(w2_scales, m), codes[:], scales[:])
             copy(result[:], acc[:])
             nc.sync.dma_start(out_rows[:, :, first : first + width], result[:])
 
-        on_scalar, on_vector = nc.scalar.copy, nc.vector.tensor_copy
-        nc.vector.tensor_tensor(z_high[:, 0, :], up[2][:, 0 : U // 2], skip_plane[2][:, 0 : U // 2], ADD)
+        whole = slice(0, CHUNK)
+        add_third(0)
         add_last(0)
         add_last(2)
-        weave(0, on_vector)
-        weave(2, on_scalar)
+        weave_lower(0)
+        weave_upper(2)
         add_last(3)
-        weave(3, on_scalar)
-        finish(0, slice(0, CHUNK), on_scalar, 5)
+        weave_upper(3)
+        finish(0, whole, nc.scalar.copy, FIRST_H_BANK)
+        add_third(1)
         add_last(1)
-        finish(2, slice(0, CHUNK), on_scalar, 6)
-        weave(1, on_vector)
-        finish(3, slice(0, CHUNK), on_scalar, 7)
-        finish(1, slice(0, CHUNK // 2), on_vector, 2)
-        finish(1, slice(CHUNK // 2, CHUNK), on_vector, 0)
+        finish(2, whole, nc.scalar.copy, FIRST_H_BANK + 1)
+        weave_lower(1)
+        finish(3, whole, nc.scalar.copy, FIRST_H_BANK + 2)
+        finish(1, slice(0, CHUNK // 2), nc.vector.tensor_copy, third_bank)
+        finish(1, slice(CHUNK // 2, CHUNK), nc.vector.tensor_copy, 0)

from contextlib import ExitStack

import concourse.mybir as mybir
from concourse.masks import make_identity

K, T, S, H, N, U = 512, 2048, 512, 512, 256, 1024
FLOPS = 2 * K * H * S + 2 * H * N * U

F32 = mybir.dt.float32
BF16 = mybir.dt.bfloat16
U32 = mybir.dt.uint32
U16 = mybir.dt.uint16
U8 = mybir.dt.uint8
FP8X4 = mybir.dt.float8_e4m3fn_x4
ADD = mybir.AluOpType.add

P = 128
PACK = 4
STRIPE = 16
HALF = S // 2
CHUNK = 256
CHUNKS = U // CHUNK
BLOCKS = CHUNK // P
LAST = PACK - 1
VECTOR_CHUNKS = (0, 1)
TENSOR_CHUNKS = (3, 2)
SPARE_BANK = CHUNKS
FIRST_H_BANK = CHUNKS + 1


def tile_picked_unet_none_e_kernel(tc, xT, w1, w2, skip, offs, cell, out):
    nc = tc.nc
    with ExitStack() as ctx:
        keep = ctx.enter_context(tc.tile_pool(name="keep", bufs=1))
        psum = ctx.enter_context(tc.psum_pool(name="psum", bufs=1))

        def bank(b, shape):
            return psum.tile([P, *shape], F32, name="bank", tag=f"bank{b}")

        def quantise(codes, scales, grouped):
            nc.vector.quantize_mx(out=codes.bitcast(FP8X4), scales=scales, in_=grouped)

        def product(acc, w_codes, w_scales, codes, scales):
            nc.tensor.matmul_mx(
                out=acc,
                lhsT=w_codes.bitcast(FP8X4),
                lhsT_scale=w_scales,
                rhs=codes.bitcast(FP8X4),
                rhs_scale=scales,
                start=True,
                stop=True,
            )

        offs_sb = keep.tile([P, S // STRIPE], U16, name="offs_sb")
        cell_sb = keep.tile([P, S // STRIPE], U16, name="cell_sb")
        x_rows = xT.rearrange("(p j) t -> j p t", j=PACK)
        skip_rows = skip.rearrange("(p j) v -> j p v", j=PACK)
        w1_halves = w1.rearrange("(p j) (h c) -> h p j c", j=PACK, h=2)
        x_plane = [keep.tile([P, T], F32, name=f"x_plane{j}") for j in range(PACK)]
        w1_raw = [keep.tile([P, PACK, H // 2], F32, name=f"w1_raw{h}") for h in range(2)]
        w2_raw = keep.tile([P, PACK, N], F32, name="w2_raw", tag="late_load")
        skip_plane = [keep.tile([P, U], F32, name=f"skip_plane{j}") for j in range(LAST)]

        nc.sync.dma_start(x_plane[0][:], x_rows[0])
        nc.sync.dma_start(offs_sb[:], offs)
        nc.sync.dma_start(cell_sb[:], cell)
        nc.sync.dma_start(w1_raw[0][:], w1_halves[0])
        for j in range(1, PACK):
            nc.sync.dma_start(x_plane[j][:], x_rows[j])
        nc.sync.dma_start(w1_raw[1][:], w1_halves[1])
        for j in range(LAST):
            nc.sync.dma_start(skip_plane[j][:], skip_rows[j])
        nc.sync.dma_start(w2_raw[:], w2.rearrange("(p j) m -> p j m", j=PACK))

        up = [keep.tile([P, U], F32, name=f"up{t}") for t in range(PACK)]
        for t in range(PACK):
            nc.vector.memset(up[t][:], 0.0)
        identity = keep.tile([P, P], F32, name="identity")
        make_identity(nc, identity[:])
        turned_low = [keep.tile([P, BLOCKS, P, 2], BF16, name=f"turned_low{c}") for c in range(CHUNKS)]
        turned_third = {
            c: keep.tile([P, BLOCKS, P, 2], BF16, name=f"turned_third{c}", tag=f"third{c}") for c in TENSOR_CHUNKS
        }
        for c in TENSOR_CHUNKS:
            nc.vector.memset(turned_third[c][:], 0.0)

        w1_low = [keep.tile([P, 2, P // 2, PACK], BF16, name=f"w1_low{h}", align_bytes=64) for h in range(2)]
        w1_high = keep.tile([P, 2, 2, P // 2, PACK], BF16, name="w1_high", align_bytes=64)
        w1_codes = keep.tile([P, H], U32, name="w1_codes", align_bytes=64)
        w1_scales = keep.tile([P, H], U8, name="w1_scales", align_bytes=64)

        def block(tile, n):
            return tile[:, n * P : (n + 1) * P]

        def deal_w1(h):
            dealt = w1_raw[h][:].rearrange("p j (r t) -> p r j t", t=PACK)
            nc.scalar.copy(out=w1_low[h][:].rearrange("p e r j -> p r j e"), in_=dealt[:, :, :, 0:2])
            nc.scalar.copy(out=w1_high[:, :, h].rearrange("p e r j -> p r j e"), in_=dealt[:, :, :, 2:4])
            quantise(block(w1_codes, h), block(w1_scales, h), w1_low[h][:].rearrange("p e r j -> p (e r j)"))

        deal_w1(0)

        x_grouped = [keep.tile([P, HALF, PACK], BF16, name=f"x_grouped{a}", align_bytes=64) for a in range(2)]
        x_codes = keep.tile([P, S], U32, name="x_codes", tag="after_x", align_bytes=64)
        x_scales = keep.tile([P, S], U8, name="x_scales", align_bytes=64)
        halves = [slice(a * HALF, (a + 1) * HALF) for a in range(2)]

        def striped(list_sb, entries):
            return list_sb[:, entries.start // STRIPE : entries.stop // STRIPE]

        for j in range(PACK):
            for a in range(2):
                nc.vector.tensor_copy(x_grouped[a][:, :, j], x_plane[j][:].indirect(striped(offs_sb, halves[a])))

        pieces = [slice(0, P), slice(P, HALF), slice(HALF, S)]
        for entries in pieces:
            a = entries.start // HALF
            grouped = x_grouped[a][:, entries.start - a * HALF : entries.stop - a * HALF, :]
            quantise(x_codes[:, entries], x_scales[:, entries], grouped.rearrange("p s j -> p (s j)"))
        deal_w1(1)
        quantise(w1_codes[:, 2 * P :], w1_scales[:, 2 * P :], w1_high[:].rearrange("p e h r j -> p (e h r j)"))

        def put(t, entries, b):
            acc = bank(b, [S])
            product(acc[:, entries], block(w1_codes, t), block(w1_scales, t), x_codes[:, entries], x_scales[:, entries])
            h_sb = keep.tile([P, entries.stop - entries.start], F32, name=f"h{t}_{entries.start}")
            nc.scalar.copy(out=h_sb[:], in_=acc[:, entries])
            nc.vector.tensor_copy(up[t][:].indirect(striped(cell_sb, entries)), h_sb[:])

        for n, entries in enumerate(pieces):
            put(0, entries, FIRST_H_BANK + n)
        for t in range(1, PACK):
            put(t, slice(0, S), FIRST_H_BANK + t - 1)

        w2_grouped = keep.tile([P, N, PACK], BF16, name="w2_grouped", tag="after_x", align_bytes=64)
        nc.scalar.copy(
            out=w2_grouped[:].rearrange("p (c i) j -> p c j i", i=PACK),
            in_=w2_raw[:].rearrange("p j (c i) -> p c j i", i=PACK),
        )
        w2_codes = keep.tile([P, N], U32, name="w2_codes", align_bytes=64)
        w2_scales = keep.tile([P, N], U8, name="w2_scales", align_bytes=64)
        quantise(w2_codes[:], w2_scales[:], w2_grouped[:].rearrange("p m j -> p (m j)"))

        skip_last = keep.tile([P, U], F32, name="skip_last", tag="late_load")
        nc.sync.dma_start(skip_last[:], skip_rows[LAST])

        cells = [slice(c * CHUNK, (c + 1) * CHUNK) for c in range(CHUNKS)]
        z_grouped = [keep.tile([P, CHUNK, PACK], BF16, name=f"z_grouped{c}", align_bytes=64) for c in range(CHUNKS)]

        def turn(dst, src, start, stop):
            nc.tensor.matmul(dst, lhsT=src, rhs=identity[:], start=start, stop=stop, is_transpose=True)

        low_sums = [bank(c, [BLOCKS, 2, 2, P // 2]) for c in range(CHUNKS)]
        for e in range(2):
            for c in range(CHUNKS):
                for g in range(BLOCKS):
                    turn(low_sums[c][:, g, :, e, :], block(skip_plane[e], BLOCKS * c + g), e == 0 and g == 0, False)
        for h in range(2):
            for c in range(CHUNKS):
                for g in range(BLOCKS):
                    columns = low_sums[c][:, g, h].rearrange("v e r -> v (e r)")
                    turn(columns, block(up[h], BLOCKS * c + g), False, h == 1 and g == BLOCKS - 1)

        third_bank = CHUNKS - 2
        pairs = []
        for c in range(CHUNKS):
            nc.scalar.copy(
                out=turned_low[c][:].rearrange("v g (h r) e -> v (g h) r e", h=2),
                in_=low_sums[c][:].rearrange("v g h e r -> v (g h) r e"),
            )
            pairs.append(bank(SPARE_BANK if c == third_bank else c, [2, CHUNK]))

        def turn_back(u, c, turned):
            words = turned[:].rearrange("v g p e -> v (g p e)").bitcast(F32)
            for g in range(BLOCKS):
                turn(pairs[c][:, u, g * P : (g + 1) * P], block(words, g), True, True)

        for c in range(CHUNKS):
            turn_back(0, c, turned_low[c])

        def z_words(c):
            return z_grouped[c][:].rearrange("p v j -> p (v j)").bitcast(F32).rearrange("p (v u) -> p v u", u=2)

        for c in VECTOR_CHUNKS:
            nc.scalar.copy(out=z_words(c)[:, :, 0], in_=pairs[c][:, 0, :])

        upper = min(TENSOR_CHUNKS)
        third_blocks = BLOCKS * len(TENSOR_CHUNKS)
        third_sums = bank(third_bank, [third_blocks, P])
        for n in range(third_blocks):
            turn(third_sums[:, n, :], block(skip_plane[2], BLOCKS * upper + n), n == 0, False)
        for n in range(third_blocks):
            turn(third_sums[:, n, :], block(up[2], BLOCKS * upper + n), False, n == third_blocks - 1)
        for c in TENSOR_CHUNKS:
            own = slice(BLOCKS * (c - upper), BLOCKS * (c - upper + 1))
            nc.scalar.copy(out=turned_third[c][:, :, :, 0], in_=third_sums[:, own, :])
        for c in TENSOR_CHUNKS:
            turn_back(1, c, turned_third[c])
        for c in TENSOR_CHUNKS:
            nc.scalar.copy(out=z_words(c), in_=pairs[c][:].rearrange("p u v -> p v u"))

        out_rows = out.rearrange("(m p) v -> p m v", p=P)
        z_lower = keep.tile([P, 2, U // 2], BF16, name="z_lower", tag=f"third{TENSOR_CHUNKS[0]}")
        z_upper = keep.tile([P, U // 2], BF16, name="z_upper", tag=f"third{TENSOR_CHUNKS[1]}")

        def add_third(c):
            nc.vector.tensor_tensor(z_lower[:, 0, cells[c]], up[2][:, cells[c]], skip_plane[2][:, cells[c]], ADD)

        def add_last(c):
            sums = z_lower[:, 1, cells[c]] if c in VECTOR_CHUNKS else z_upper[:, cells[c - upper]]
            nc.vector.tensor_tensor(sums, up[LAST][:, cells[c]], skip_last[:, cells[c]], ADD)

        def weave_lower(c):
            nc.vector.tensor_copy(z_grouped[c][:, :, 2:4], z_lower[:, :, cells[c]].rearrange("p e v -> p v e"))

        def weave_upper(c):
            nc.scalar.copy(out=z_grouped[c][:, :, LAST], in_=z_upper[:, cells[c - upper]])

        def finish(c, part, copy, b):
            width = part.stop - part.start
            first = cells[c].start + part.start
            codes = keep.tile([P, width], U32, name=f"z_codes{first}", align_bytes=64)
            scales = keep.tile([P, width], U8, name=f"z_scales{first}", align_bytes=64)
            quantise(codes[:], scales[:], z_grouped[c][:, part, :].rearrange("p v j -> p (v j)"))
            result = keep.tile([P, N // P, width], F32, name=f"result{first}")
            acc = bank(b, [N // P, width])
            for m in range(N // P):
                product(acc[:, m, :], block(w2_codes, m), block(w2_scales, m), codes[:], scales[:])
            copy(result[:], acc[:])
            nc.sync.dma_start(out_rows[:, :, first : first + width], result[:])

        whole = slice(0, CHUNK)
        add_third(0)
        add_last(0)
        add_last(2)
        weave_lower(0)
        weave_upper(2)
        add_last(3)
        weave_upper(3)
        finish(0, whole, nc.scalar.copy, FIRST_H_BANK)
        add_third(1)
        add_last(1)
        finish(2, whole, nc.scalar.copy, FIRST_H_BANK + 1)
        weave_lower(1)
        finish(3, whole, nc.scalar.copy, FIRST_H_BANK + 2)
        finish(1, slice(0, CHUNK // 2), nc.vector.tensor_copy, third_bank)
        finish(1, slice(CHUNK // 2, CHUNK), nc.vector.tensor_copy, 0)
